import numpy as np
import ml_dtypes


def mxq(x, axis, fmt="e4m3"):
    dtype, down = {"e4m3": (ml_dtypes.float8_e4m3fn, 7), "e5m2": (ml_dtypes.float8_e5m2, 14)}[fmt]
    v = np.moveaxis(np.asarray(x, np.float32).astype(ml_dtypes.bfloat16).astype(np.float64), axis, -1)
    blocks = v.reshape(v.shape[:-1] + (-1, 32))
    amax = np.abs(blocks).max(-1, keepdims=True)
    byte = np.maximum(np.where(amax > 0, np.frexp(amax)[1] - 1 + 127, 0) - down, 1)
    scale = np.exp2(byte - 127.0)
    codes = (blocks / scale).astype(np.float32).astype(dtype).astype(np.float64)
    return np.moveaxis((codes * scale).reshape(v.shape), -1, axis)


WIDE = False


def mx_kscale(k):
    if not WIDE:
        return np.ones(k)
    levels = np.array([10, -10, 5, -5, 0])
    if k % 512:
        return np.exp2(np.random.permutation(np.resize(levels, k // 32))).repeat(32)
    a = np.empty((k // 512, 16))
    for p in range(k // 512):
        a[p, :8] = np.random.permutation(np.resize(levels, 8))
        for g in range(8):
            far = levels[np.abs(levels - a[p, g]) >= 10]
            a[p, g + 8] = far[np.random.randint(len(far))]
    return np.exp2(a.ravel()).repeat(32)


def f64(x):
    return np.asarray(x).astype(np.float64)


def striped(idx):
    return np.tile(idx.reshape(-1, 16).T, (8, 1)).astype(np.uint16)


def unstriped(offs):
    return offs[:16].T.reshape(-1).astype(np.int64)


def striped8(idx):
    return np.concatenate([x.reshape(-1, 16).T for x in idx]).astype(np.uint16)


def runs(offs, k):
    lists = np.stack([offs[16 * r : 16 * r + 16].T.reshape(-1) for r in range(8)]).astype(np.int64)
    return lists[np.arange(k) % 512 // 64]


def pack_weight(w):
    k, n = w.shape
    w = f64(np.asarray(w, np.float32).astype(ml_dtypes.bfloat16)).reshape(k // 32, 32, n)
    amax = np.abs(w).max(1)
    byte = np.clip(np.where(amax > 0, np.frexp(amax)[1] - 1 + 127 - 7, 1), 1, 254)
    scaled = (w * np.exp2(127.0 - byte)[:, None, :]).reshape(k, n).astype(np.float32)
    words = np.ascontiguousarray(scaled.reshape(k // 512, 128, 4, n).transpose(0, 1, 3, 2)).astype(ml_dtypes.float8_e4m3fn).view(np.uint8)
    return words, np.ascontiguousarray(byte.astype(np.uint8).reshape(k // 512, 16, n))


def unpack_weight(words, scales):
    g, p, n, _ = words.shape
    vals = np.ascontiguousarray(words).view(ml_dtypes.float8_e4m3fn).astype(np.float64) * np.repeat(np.exp2(scales.astype(np.float64) - 127.0), 8, axis=1)[..., None]
    return vals.transpose(0, 1, 3, 2).reshape(g * 512, n)


def sigmoid(v):
    return 1.0 / (1.0 + np.exp(-np.maximum(v, -700.0)))

def planes(y):
    n, m = y.shape
    v = y.astype(np.float32).astype(ml_dtypes.bfloat16).astype(np.float64).reshape(n // 32, 32, m)
    top = np.abs(v).max(1)
    byte = np.clip(np.where(top > 0, np.frexp(top)[1] - 1 + 127 - 7, 1), 1, 254)
    codes = (v * np.exp2(127.0 - byte)[:, None, :]).reshape(n, m).astype(np.float32).astype(ml_dtypes.float8_e4m3fn).view(np.uint8)
    words = codes.reshape(n // 512, 128, 4, m).transpose(0, 1, 3, 2)
    return np.ascontiguousarray(words), np.ascontiguousarray(byte.astype(np.uint8).reshape(n // 512, 16, m))


K, T, S, H, W, G = 512, 2048, 512, 512, 256, 2048


def setup_inputs():
    n = np.random.standard_normal
    s = mx_kscale(K)[:, None]
    packed_xT = pack_weight(n((K, T)) * s)
    packed_w1 = pack_weight(n((K, H)) / np.sqrt(K) / s)
    packed_dT = pack_weight(n((K, G)) / s)
    perm = np.stack([np.random.permutation(S) for _ in range(8)])
    return {
        "x_words": packed_xT[0],
        "x_scales": packed_xT[1],
        "w1_words": packed_w1[0],
        "w1_scales": packed_w1[1],
        "gs": (np.random.uniform(0.5, 1.5, (K, 1)) * s).astype(np.float32),
        "d_words": packed_dT[0],
        "d_scales": packed_dT[1],
        "offs": striped(np.random.permutation(T)[:S]),
        "n1": striped8(perm[:, :W]),
        "n2": striped8(perm[:, W:]),
        "k1": striped8(np.random.randint(0, G, (8, H))),
        "n3": striped8(np.stack([np.random.permutation(S) for _ in range(8)])),
        "n4": striped8(np.stack([np.random.permutation(S) for _ in range(8)])),
    }


def reference(x_words, x_scales, w1_words, w1_scales, gs, d_words, d_scales, offs, n1, n2, k1, n3, n4):
    d_k1 = unpack_weight(d_words, d_scales)[np.arange(K)[:, None], runs(k1, K)]
    xq = unpack_weight(x_words, x_scales)[:, unstriped(offs)]
    y = unpack_weight(w1_words, w1_scales).T @ xq
    pa = y[np.arange(H)[:, None], runs(n1, H)]
    pb = y[np.arange(H)[:, None], runs(n2, H)]
    rb = pa - pb
    ra = 0.75 * (pa + pb)
    ds = np.zeros((H, S))
    ds[np.arange(H)[:, None], runs(n1, H)] = ra
    dt = ds.copy()
    dt[np.arange(H)[:, None], runs(n2, H)] = rb
    z = f64(gs) * dt
    h = 0.0625 * ((d_k1.T @ mxq(z, 0, "e4m3")))
    out_0 = (h - (h[np.arange(H)[:, None], runs(n3, H)])) * (sigmoid(h[np.arange(H)[:, None], runs(n4, H)]))
    return (out_0,) + planes(out_0)

@@ -1,0 +1,196 @@
+from contextlib import ExitStack
+
+import concourse.mybir as mybir
+
+K, T, S, H, W, G = 512, 2048, 512, 512, 256, 2048
+FLOPS = 2 * K * H * S * 2
+
+F32 = mybir.dt.float32
+BF16 = mybir.dt.bfloat16
+I32 = mybir.dt.int32
+U32 = mybir.dt.uint32
+U16 = mybir.dt.uint16
+U8 = mybir.dt.uint8
+FP8X4 = mybir.dt.float8_e4m3fn_x4
+MULT = mybir.AluOpType.mult
+ADD = mybir.AluOpType.add
+SUB = mybir.AluOpType.subtract
+COPY = mybir.ActivationFunctionType.Copy
+SIGMOID = mybir.ActivationFunctionType.Sigmoid
+
+P = 128
+PACK = 4
+HALF = S // 2
+LCOL = HALF // 16
+
+
+def tile_picked_densehaargdif_none_po_kernel(tc, x_words, x_scales, w1_words, w1_scales, gs, d_words, d_scales, offs, n1, n2, k1, n3, n4, out_0, out_1, out_2):
+    nc = tc.nc
+    with ExitStack() as ctx:
+        sb = ctx.enter_context(tc.tile_pool(name="sb", bufs=1))
+        ps = ctx.enter_context(tc.psum_pool(name="ps", bufs=1))
+
+        def words(ap):
+            return ap[0].rearrange("p n t -> p (n t)").bitcast(I32)
+
+        def sbt(name, shape, dtype, tag=None):
+            return sb.tile(shape, dtype, name=name, tag=tag or name, align_bytes=64)
+
+        def halfc(c):
+            return slice(c * HALF, (c + 1) * HALF)
+
+        lists = {}
+
+        def load_list(name, ap):
+            lists[name] = sb.tile(list(ap.shape), U16, name="list_" + name)
+            nc.sync.dma_start(lists[name][:], ap)
+
+        xs = sbt("xs", [P, T], U8)
+        ws = sbt("ws", [P, H], U8)
+        dsc = sbt("dsc", [P, G], U8)
+        dks = sbt("dks", [P, H], U8)
+        c075 = sbt("c075", [P, W], F32)
+        nc.gpsimd.memset(xs[:].bitcast(I32), 0)
+        nc.vector.memset(ws[:].bitcast(I32), 0)
+        nc.vector.memset(dsc[:].bitcast(I32), 0)
+        nc.vector.memset(c075[:], 0.75)
+        nc.vector.memset(dks[:].bitcast(I32), 0)
+
+        xw = sbt("xw", [P, T], I32)
+        ww = sbt("ww", [P, H], I32)
+        gst = sbt("gst", [P, PACK], F32)
+
+        load_list("offs", offs)
+        nc.sync.dma_start(ww[:], words(w1_words))
+        for r in range(4):
+            nc.sync.dma_start(xs[r:P:32, :].bitcast(I32), x_scales[0, r:16:4, :].bitcast(I32))
+        nc.sync.dma_start(xw[:], words(x_words))
+        for r in range(4):
+            nc.sync.dma_start(ws[r:P:32, :].bitcast(I32), w1_scales[0, r:16:4, :].bitcast(I32))
+        load_list("k1", k1)
+        for b in range(2):
+            nc.sync.dma_start(dsc[b:P:16, :].bitcast(I32), d_scales[0, b:16:2, :].bitcast(I32))
+        load_list("n2", n2)
+        load_list("n1", n1)
+        nc.sync.dma_start(gst[:], gs.rearrange("(p t) o -> p (t o)", t=PACK))
+        load_list("n3", n3)
+        load_list("n4", n4)
+
+        warm = sbt("warm", [P, 1], F32)
+        nc.scalar.activation(warm[:], c075[:, 0:1], SIGMOID)
+
+        def deal(dst, src):
+            nc.vector.tensor_copy(dst.rearrange("p (t m) -> p t m", t=PACK), src.rearrange("p (m t) -> p t m", t=PACK))
+
+        wwd = sbt("wwd", [P, H], I32)
+        wsd = sbt("wsd", [P, H], U8)
+        deal(wwd[:], ww[:])
+        xsg = sbt("xsg", [P, S], U8)
+        nc.vector.tensor_copy(xsg[:], xs[:].indirect(lists["offs"][:]))
+        xwg = sbt("xwg", [P, S], I32)
+        for c in range(2):
+            nc.vector.tensor_copy(xwg[:, halfc(c)].bitcast(U32), xw[:].bitcast(U32).indirect(lists["offs"][:, c * LCOL : (c + 1) * LCOL]))
+            if c == 0:
+                deal(wsd[:], ws[:])
+
+        def product(name, lw, ls, rw, rs, order):
+            res = {}
+            for t, c in order:
+                acc = ps.tile([P, HALF], F32, name=f"{name}{t}{c}", tag=f"bank{2 * t + c}")
+                m = slice(t * P, (t + 1) * P)
+                nc.tensor.matmul_mx(out=acc[:], lhsT=lw[:, m].bitcast(FP8X4), lhsT_scale=ls[:, m], rhs=rw[:, halfc(c)].bitcast(FP8X4), rhs_scale=rs[:, halfc(c)], start=True, stop=True)
+                res[t, c] = acc
+            return res
+
+        order = [(t, c) for t in range(PACK) for c in range(2)]
+        yp = product("yp", wwd, wsd, xwg, xsg, order)
+
+        dw = sbt("dw", [P, G], I32, tag="xwg")
+        nc.sync.dma_start(dw[:], words(d_words))
+        dsg = sbt("dsg", [P, H], U8, tag="xw")
+        dsd = sbt("dsd", [P, H], U8)
+        nc.vector.tensor_copy(dsg[:], dsc[:].indirect(lists["k1"][:]))
+        deal(dsd[:], dsg[:])
+        for r in range(4):
+            src = 16 * (r // 2) + r % 2
+            nc.sync.dma_start(dks[r:P:32, :].bitcast(I32), dsd[src:P:32, :].bitcast(I32))
+
+        y = [sbt(f"y{t}", [P, S], F32) for t in range(PACK)]
+        for t in range(PACK):
+            for c in range(2):
+                nc.scalar.activation(y[t][:, halfc(c)], yp[t, c][:], COPY)
+
+        zb = sbt("zb", [P, S, PACK], BF16)
+        pb, sm, m2, dt = {}, {}, {}, {}
+
+        def gathers(t):
+            pb[t] = sbt(f"pb{t}", [P, W], F32)
+            sm[t] = sbt(f"sm{t}", [P, W], F32)
+            m2[t] = sbt(f"m2{t}", [P, W], F32)
+            nc.vector.tensor_copy(pb[t][:], y[t][:].indirect(lists["n2"][:]))
+            nc.scalar.activation(m2[t][:], pb[t][:], COPY, scale=-2.0)
+
+        def gathers2(t):
+            nc.vector.tensor_tensor(sm[t][:], y[t][:].indirect(lists["n1"][:]), pb[t][:], ADD)
+
+        def scat1(t):
+            dt[t] = sbt(f"dt{t}", [P, S], F32)
+            nc.vector.tensor_tensor(dt[t][:].indirect(lists["n1"][:]), sm[t][:], c075[:], MULT)
+
+        def scat2(t):
+            nc.vector.tensor_tensor(dt[t][:].indirect(lists["n2"][:]), sm[t][:], m2[t][:], ADD)
+            for c in range(2):
+                nc.scalar.activation(zb[:, halfc(c), t], dt[t][:, halfc(c)], COPY, scale=gst[:, t : t + 1])
+
+        for t0 in (0, 2):
+            for step in (gathers, gathers2, scat1, scat2):
+                step(t0)
+                step(t0 + 1)
+
+        dwg = sbt("dwg", [P, H], I32, tag="sm3")
+        dwd = sbt("dwd", [P, H], I32)
+        nc.vector.tensor_copy(dwg[:].bitcast(U32), dw[:].bitcast(U32).indirect(lists["k1"][:]))
+        deal(dwd[:], dwg[:])
+
+        zw = sbt("zw", [P, S], I32)
+        zs = sbt("zs", [P, S], U8)
+        for c in range(2):
+            nc.vector.quantize_mx(out=zw[:, halfc(c)].bitcast(FP8X4), scales=zs[:, halfc(c)], in_=zb[:, halfc(c), :].rearrange("p n t -> p (n t)"))
+        hp = product("hp", dwd, dks, zw, zs, order)
+
+        h = [sbt(f"h{t}", [P, S], F32) for t in range(PACK)]
+        h2 = {(t, c): sbt(f"hh{t}{c}", [P, HALF], F32) for t in range(PACK) for c in range(2)}
+        for t in range(PACK):
+            for c in range(2):
+                nc.scalar.activation(h[t][:, halfc(c)], hp[t, c][:], COPY, scale=0.0625)
+            nc.sync.dma_start(h2[t, 1][:], h[t][:, halfc(1)])
+        sig = sbt("sig", [P, PACK, S], F32)
+        dif = sbt("dif", [P, PACK, S], F32)
+        o = sbt("o", [P, PACK, S], F32)
+        ob = sbt("ob", [P, S, PACK], BF16)
+        ow = sbt("ow", [P, S], I32)
+        osc = sbt("osc", [P, S], U8)
+        out_rows = out_0.rearrange("(p t) c -> p t c", t=PACK)
+
+        def interleave(eng_copy, cols):
+            eng_copy(ob[:, cols, :].rearrange("p (c i) t -> p c t i", i=4), o[:, :, cols].rearrange("p t (c i) -> p c t i", i=4))
+
+        for c in range(2):
+            lc = slice(c * LCOL, (c + 1) * LCOL)
+            for t in range(PACK):
+                nc.scalar.activation(sig[:, t, halfc(c)], h[t][:].indirect(lists["n4"][:, lc]), SIGMOID)
+                if c == 0:
+                    nc.vector.tensor_copy(h2[t, 0][:], h[t][:, halfc(0)])
+                nc.vector.tensor_tensor(dif[:, t, halfc(c)], h[t][:].indirect(lists["n3"][:, lc]), h2[t, c][:], SUB)
+            for t in range(PACK):
+                nc.vector.scalar_tensor_tensor(o[:, t, halfc(c)], dif[:, t, halfc(c)], -1.0, sig[:, t, halfc(c)], MULT, MULT)
+                nc.sync.dma_start(out_rows[:, t, halfc(c)], o[:, t, halfc(c)])
+        interleave(nc.scalar.copy, halfc(0))
+        interleave(nc.scalar.copy, slice(HALF, HALF + 96))
+        interleave(nc.vector.tensor_copy, slice(HALF + 96, S))
+        for c in range(2):
+            nc.vector.quantize_mx(out=ow[:, halfc(c)].bitcast(FP8X4), scales=osc[:, halfc(c)], in_=ob[:, halfc(c), :].rearrange("p n t -> p (n t)"))
+            nc.sync.dma_start(words(out_1)[:, halfc(c)], ow[:, halfc(c)])
+        for r in range(4):
+            eng = nc.scalar if r % 2 else nc.sync
+            eng.dma_start(out_2[0, r:16:4, :].bitcast(I32), osc[r:P:32, :].bitcast(I32))

@@ -51,9 +51,9 @@ def tile_picked_densehaargdif_none_po_kernel(tc, x_words, x_scales, w1_words, w1
         dks = sbt("dks", [P, H], U8)
         c075 = sbt("c075", [P, W], F32)
         nc.gpsimd.memset(xs[:].bitcast(I32), 0)
+        nc.gpsimd.memset(c075[:], 0.75)
         nc.vector.memset(ws[:].bitcast(I32), 0)
         nc.vector.memset(dsc[:].bitcast(I32), 0)
-        nc.vector.memset(c075[:], 0.75)
         nc.vector.memset(dks[:].bitcast(I32), 0)
 
         xw = sbt("xw", [P, T], I32)
@@ -63,7 +63,8 @@ def tile_picked_densehaargdif_none_po_kernel(tc, x_words, x_scales, w1_words, w1
         load_list("offs", offs)
         nc.sync.dma_start(ww[:], words(w1_words))
         for r in range(4):
-            nc.sync.dma_start(xs[r:P:32, :].bitcast(I32), x_scales[0, r:16:4, :].bitcast(I32))
+            eng = nc.scalar if r % 2 else nc.sync
+            eng.dma_start(xs[r:P:32, :].bitcast(I32), x_scales[0, r:16:4, :].bitcast(I32))
         nc.sync.dma_start(xw[:], words(x_words))
         for r in range(4):
             nc.sync.dma_start(ws[r:P:32, :].bitcast(I32), w1_scales[0, r:16:4, :].bitcast(I32))
@@ -79,19 +80,19 @@ def tile_picked_densehaargdif_none_po_kernel(tc, x_words, x_scales, w1_words, w1
         warm = sbt("warm", [P, 1], F32)
         nc.scalar.activation(warm[:], c075[:, 0:1], SIGMOID)
 
-        def deal(dst, src):
-            nc.vector.tensor_copy(dst.rearrange("p (t m) -> p t m", t=PACK), src.rearrange("p (m t) -> p t m", t=PACK))
+        def deal(dst, src, run):
+            nc.vector.tensor_copy(dst.rearrange("p (t a i) -> p a t i", t=PACK, i=run), src.rearrange("p (a i t) -> p a t i", t=PACK, i=run))
 
         wwd = sbt("wwd", [P, H], I32)
         wsd = sbt("wsd", [P, H], U8)
-        deal(wwd[:], ww[:])
+        deal(wwd[:], ww[:], 4)
         xsg = sbt("xsg", [P, S], U8)
         nc.vector.tensor_copy(xsg[:], xs[:].indirect(lists["offs"][:]))
         xwg = sbt("xwg", [P, S], I32)
         for c in range(2):
             nc.vector.tensor_copy(xwg[:, halfc(c)].bitcast(U32), xw[:].bitcast(U32).indirect(lists["offs"][:, c * LCOL : (c + 1) * LCOL]))
             if c == 0:
-                deal(wsd[:], ws[:])
+                deal(wsd[:], ws[:], 16)
 
         def product(name, lw, ls, rw, rs, order):
             res = {}
@@ -108,12 +109,7 @@ def tile_picked_densehaargdif_none_po_kernel(tc, x_words, x_scales, w1_words, w1
         dw = sbt("dw", [P, G], I32, tag="xwg")
         nc.sync.dma_start(dw[:], words(d_words))
         dsg = sbt("dsg", [P, H], U8, tag="xw")
-        dsd = sbt("dsd", [P, H], U8)
         nc.vector.tensor_copy(dsg[:], dsc[:].indirect(lists["k1"][:]))
-        deal(dsd[:], dsg[:])
-        for r in range(4):
-            src = 16 * (r // 2) + r % 2
-            nc.sync.dma_start(dks[r:P:32, :].bitcast(I32), dsd[src:P:32, :].bitcast(I32))
 
         y = [sbt(f"y{t}", [P, S], F32) for t in range(PACK)]
         for t in range(PACK):
@@ -142,20 +138,30 @@ def tile_picked_densehaargdif_none_po_kernel(tc, x_words, x_scales, w1_words, w1
             for c in range(2):
                 nc.scalar.activation(zb[:, halfc(c), t], dt[t][:, halfc(c)], COPY, scale=gst[:, t : t + 1])
 
+        def d_scale_rows():
+            dsd = sbt("dsd", [P, H], U8, tag="pb0")
+            deal(dsd[:], dsg[:], 16)
+            for r in range(4):
+                src = 16 * (r // 2) + r % 2
+                nc.sync.dma_start(dks[r:P:32, :].bitcast(I32), dsd[src:P:32, :].bitcast(I32))
+
         for t0 in (0, 2):
             for step in (gathers, gathers2, scat1, scat2):
                 step(t0)
                 step(t0 + 1)
+                if t0 == 0 and step == gathers2:
+                    d_scale_rows()
 
         dwg = sbt("dwg", [P, H], I32, tag="sm3")
         dwd = sbt("dwd", [P, H], I32)
         nc.vector.tensor_copy(dwg[:].bitcast(U32), dw[:].bitcast(U32).indirect(lists["k1"][:]))
-        deal(dwd[:], dwg[:])
 
         zw = sbt("zw", [P, S], I32)
         zs = sbt("zs", [P, S], U8)
         for c in range(2):
             nc.vector.quantize_mx(out=zw[:, halfc(c)].bitcast(FP8X4), scales=zs[:, halfc(c)], in_=zb[:, halfc(c), :].rearrange("p n t -> p (n t)"))
+            if c == 0:
+                deal(dwd[:], dwg[:], 4)
         hp = product("hp", dwd, dks, zw, zs, order)
 
         h = [sbt(f"h{t}", [P, S], F32) for t in range(PACK)]
@@ -163,34 +169,42 @@ def tile_picked_densehaargdif_none_po_kernel(tc, x_words, x_scales, w1_words, w1
         for t in range(PACK):
             for c in range(2):
                 nc.scalar.activation(h[t][:, halfc(c)], hp[t, c][:], COPY, scale=0.0625)
+            if t >= 2:
+                nc.scalar.activation(h2[t, 0][:], hp[t, 0][:], COPY, scale=0.0625)
             nc.sync.dma_start(h2[t, 1][:], h[t][:, halfc(1)])
         sig = sbt("sig", [P, PACK, S], F32)
         dif = sbt("dif", [P, PACK, S], F32)
         o = sbt("o", [P, PACK, S], F32)
-        ob = sbt("ob", [P, S, PACK], BF16)
-        ow = sbt("ow", [P, S], I32)
         osc = sbt("osc", [P, S], U8)
         out_rows = out_0.rearrange("(p t) c -> p t c", t=PACK)
-
-        def interleave(eng_copy, cols):
-            eng_copy(ob[:, cols, :].rearrange("p (c i) t -> p c t i", i=4), o[:, :, cols].rearrange("p t (c i) -> p c t i", i=4))
 
         for c in range(2):
             lc = slice(c * LCOL, (c + 1) * LCOL)
             for t in range(PACK):
                 nc.scalar.activation(sig[:, t, halfc(c)], h[t][:].indirect(lists["n4"][:, lc]), SIGMOID)
-                if c == 0:
+                tv = (t - c) % PACK
+                if c == 0 and t < 2:
                     nc.vector.tensor_copy(h2[t, 0][:], h[t][:, halfc(0)])
-                nc.vector.tensor_tensor(dif[:, t, halfc(c)], h[t][:].indirect(lists["n3"][:, lc]), h2[t, c][:], SUB)
+                nc.vector.tensor_tensor(dif[:, tv, halfc(c)], h[tv][:].indirect(lists["n3"][:, lc]), h2[tv, c][:], SUB)
             for t in range(PACK):
                 nc.vector.scalar_tensor_tensor(o[:, t, halfc(c)], dif[:, t, halfc(c)], -1.0, sig[:, t, halfc(c)], MULT, MULT)
                 nc.sync.dma_start(out_rows[:, t, halfc(c)], o[:, t, halfc(c)])
-        interleave(nc.scalar.copy, halfc(0))
-        interleave(nc.scalar.copy, slice(HALF, HALF + 96))
-        interleave(nc.vector.tensor_copy, slice(HALF + 96, S))
-        for c in range(2):
-            nc.vector.quantize_mx(out=ow[:, halfc(c)].bitcast(FP8X4), scales=osc[:, halfc(c)], in_=ob[:, halfc(c), :].rearrange("p n t -> p (n t)"))
+        ob = [sbt("ob0", [P, HALF, PACK], BF16, tag="h3"), sbt("ob1", [P, HALF, PACK], BF16)]
+
+        def interleave(copy, c, lo, hi):
+            copy(ob[c][:, lo:hi, :].rearrange("p (c i) t -> p c t i", i=4), o[:, :, c * HALF + lo : c * HALF + hi].rearrange("p t (c i) -> p c t i", i=4))
+
+        ow = sbt("ow", [P, S], I32)
+
+        def planes(c):
+            nc.vector.quantize_mx(out=ow[:, halfc(c)].bitcast(FP8X4), scales=osc[:, halfc(c)], in_=ob[c][:].rearrange("p n t -> p (n t)"))
             nc.sync.dma_start(words(out_1)[:, halfc(c)], ow[:, halfc(c)])
+
+        interleave(nc.scalar.copy, 0, 0, HALF)
+        interleave(nc.scalar.copy, 1, 0, 64)
+        interleave(nc.vector.tensor_copy, 1, 64, HALF)
+        planes(0)
+        planes(1)
         for r in range(4):
-            eng = nc.scalar if r % 2 else nc.sync
+            eng = nc.sync if r == 3 else nc.scalar
             eng.dma_start(out_2[0, r:16:4, :].bitcast(I32), osc[r:P:32, :].bitcast(I32))

from contextlib import ExitStack

import concourse.mybir as mybir

K, T, S, H, W, G = 512, 2048, 512, 512, 256, 2048
FLOPS = 2 * K * H * S * 2

F32 = mybir.dt.float32
BF16 = mybir.dt.bfloat16
I32 = mybir.dt.int32
U32 = mybir.dt.uint32
U16 = mybir.dt.uint16
U8 = mybir.dt.uint8
FP8X4 = mybir.dt.float8_e4m3fn_x4
MULT = mybir.AluOpType.mult
ADD = mybir.AluOpType.add
SUB = mybir.AluOpType.subtract
COPY = mybir.ActivationFunctionType.Copy
SIGMOID = mybir.ActivationFunctionType.Sigmoid

P = 128
PACK = 4
HALF = S // 2
LCOL = HALF // 16


def tile_picked_densehaargdif_none_po_kernel(tc, x_words, x_scales, w1_words, w1_scales, gs, d_words, d_scales, offs, n1, n2, k1, n3, n4, out_0, out_1, out_2):
    nc = tc.nc
    with ExitStack() as ctx:
        sb = ctx.enter_context(tc.tile_pool(name="sb", bufs=1))
        ps = ctx.enter_context(tc.psum_pool(name="ps", bufs=1))

        def words(ap):
            return ap[0].rearrange("p n t -> p (n t)").bitcast(I32)

        def sbt(name, shape, dtype, tag=None):
            return sb.tile(shape, dtype, name=name, tag=tag or name, align_bytes=64)

        def halfc(c):
            return slice(c * HALF, (c + 1) * HALF)

        lists = {}

        def load_list(name, ap):
            lists[name] = sb.tile(list(ap.shape), U16, name="list_" + name)
            nc.sync.dma_start(lists[name][:], ap)

        xs = sbt("xs", [P, T], U8)
        ws = sbt("ws", [P, H], U8)
        dsc = sbt("dsc", [P, G], U8)
        dks = sbt("dks", [P, H], U8)
        c075 = sbt("c075", [P, W], F32)
        nc.gpsimd.memset(xs[:].bitcast(I32), 0)
        nc.gpsimd.memset(c075[:], 0.75)
        nc.vector.memset(ws[:].bitcast(I32), 0)
        nc.vector.memset(dsc[:].bitcast(I32), 0)
        nc.vector.memset(dks[:].bitcast(I32), 0)

        xw = sbt("xw", [P, T], I32)
        ww = sbt("ww", [P, H], I32)
        gst = sbt("gst", [P, PACK], F32)

        load_list("offs", offs)
        nc.sync.dma_start(ww[:], words(w1_words))
        for r in range(4):
            eng = nc.scalar if r % 2 else nc.sync
            eng.dma_start(xs[r:P:32, :].bitcast(I32), x_scales[0, r:16:4, :].bitcast(I32))
        nc.sync.dma_start(xw[:], words(x_words))
        for r in range(4):
            nc.sync.dma_start(ws[r:P:32, :].bitcast(I32), w1_scales[0, r:16:4, :].bitcast(I32))
        load_list("k1", k1)
        for b in range(2):
            nc.sync.dma_start(dsc[b:P:16, :].bitcast(I32), d_scales[0, b:16:2, :].bitcast(I32))
        load_list("n2", n2)
        load_list("n1", n1)
        nc.sync.dma_start(gst[:], gs.rearrange("(p t) o -> p (t o)", t=PACK))
        load_list("n3", n3)
        load_list("n4", n4)

        warm = sbt("warm", [P, 1], F32)
        nc.scalar.activation(warm[:], c075[:, 0:1], SIGMOID)

        def deal(dst, src, run):
            nc.vector.tensor_copy(dst.rearrange("p (t a i) -> p a t i", t=PACK, i=run), src.rearrange("p (a i t) -> p a t i", t=PACK, i=run))

        wwd = sbt("wwd", [P, H], I32)
        wsd = sbt("wsd", [P, H], U8)
        deal(wwd[:], ww[:], 4)
        xsg = sbt("xsg", [P, S], U8)
        nc.vector.tensor_copy(xsg[:], xs[:].indirect(lists["offs"][:]))
        xwg = sbt("xwg", [P, S], I32)
        for c in range(2):
            nc.vector.tensor_copy(xwg[:, halfc(c)].bitcast(U32), xw[:].bitcast(U32).indirect(lists["offs"][:, c * LCOL : (c + 1) * LCOL]))
            if c == 0:
                deal(wsd[:], ws[:], 16)

        def product(name, lw, ls, rw, rs, order):
            res = {}
            for t, c in order:
                acc = ps.tile([P, HALF], F32, name=f"{name}{t}{c}", tag=f"bank{2 * t + c}")
                m = slice(t * P, (t + 1) * P)
                nc.tensor.matmul_mx(out=acc[:], lhsT=lw[:, m].bitcast(FP8X4), lhsT_scale=ls[:, m], rhs=rw[:, halfc(c)].bitcast(FP8X4), rhs_scale=rs[:, halfc(c)], start=True, stop=True)
                res[t, c] = acc
            return res

        order = [(t, c) for t in range(PACK) for c in range(2)]
        yp = product("yp", wwd, wsd, xwg, xsg, order)

        dw = sbt("dw", [P, G], I32, tag="xwg")
        nc.sync.dma_start(dw[:], words(d_words))
        dsg = sbt("dsg", [P, H], U8, tag="xw")
        nc.vector.tensor_copy(dsg[:], dsc[:].indirect(lists["k1"][:]))

        y = [sbt(f"y{t}", [P, S], F32) for t in range(PACK)]
        for t in range(PACK):
            for c in range(2):
                nc.scalar.activation(y[t][:, halfc(c)], yp[t, c][:], COPY)

        zb = sbt("zb", [P, S, PACK], BF16)
        pb, sm, m2, dt = {}, {}, {}, {}

        def gathers(t):
            pb[t] = sbt(f"pb{t}", [P, W], F32)
            sm[t] = sbt(f"sm{t}", [P, W], F32)
            m2[t] = sbt(f"m2{t}", [P, W], F32)
            nc.vector.tensor_copy(pb[t][:], y[t][:].indirect(lists["n2"][:]))
            nc.scalar.activation(m2[t][:], pb[t][:], COPY, scale=-2.0)

        def gathers2(t):
            nc.vector.tensor_tensor(sm[t][:], y[t][:].indirect(lists["n1"][:]), pb[t][:], ADD)

        def scat1(t):
            dt[t] = sbt(f"dt{t}", [P, S], F32)
            nc.vector.tensor_tensor(dt[t][:].indirect(lists["n1"][:]), sm[t][:], c075[:], MULT)

        def scat2(t):
            nc.vector.tensor_tensor(dt[t][:].indirect(lists["n2"][:]), sm[t][:], m2[t][:], ADD)
            for c in range(2):
                nc.scalar.activation(zb[:, halfc(c), t], dt[t][:, halfc(c)], COPY, scale=gst[:, t : t + 1])

        def d_scale_rows():
            dsd = sbt("dsd", [P, H], U8, tag="pb0")
            deal(dsd[:], dsg[:], 16)
            for r in range(4):
                src = 16 * (r // 2) + r % 2
                nc.sync.dma_start(dks[r:P:32, :].bitcast(I32), dsd[src:P:32, :].bitcast(I32))

        for t0 in (0, 2):
            for step in (gathers, gathers2, scat1, scat2):
                step(t0)
                step(t0 + 1)
                if t0 == 0 and step == gathers2:
                    d_scale_rows()

        dwg = sbt("dwg", [P, H], I32, tag="sm3")
        dwd = sbt("dwd", [P, H], I32)
        nc.vector.tensor_copy(dwg[:].bitcast(U32), dw[:].bitcast(U32).indirect(lists["k1"][:]))

        zw = sbt("zw", [P, S], I32)
        zs = sbt("zs", [P, S], U8)
        for c in range(2):
            nc.vector.quantize_mx(out=zw[:, halfc(c)].bitcast(FP8X4), scales=zs[:, halfc(c)], in_=zb[:, halfc(c), :].rearrange("p n t -> p (n t)"))
            if c == 0:
                deal(dwd[:], dwg[:], 4)
        hp = product("hp", dwd, dks, zw, zs, order)

        h = [sbt(f"h{t}", [P, S], F32) for t in range(PACK)]
        h2 = {(t, c): sbt(f"hh{t}{c}", [P, HALF], F32) for t in range(PACK) for c in range(2)}
        for t in range(PACK):
            for c in range(2):
                nc.scalar.activation(h[t][:, halfc(c)], hp[t, c][:], COPY, scale=0.0625)
            if t >= 2:
                nc.scalar.activation(h2[t, 0][:], hp[t, 0][:], COPY, scale=0.0625)
            nc.sync.dma_start(h2[t, 1][:], h[t][:, halfc(1)])
        sig = sbt("sig", [P, PACK, S], F32)
        dif = sbt("dif", [P, PACK, S], F32)
        o = sbt("o", [P, PACK, S], F32)
        osc = sbt("osc", [P, S], U8)
        out_rows = out_0.rearrange("(p t) c -> p t c", t=PACK)

        for c in range(2):
            lc = slice(c * LCOL, (c + 1) * LCOL)
            for t in range(PACK):
                nc.scalar.activation(sig[:, t, halfc(c)], h[t][:].indirect(lists["n4"][:, lc]), SIGMOID)
                tv = (t - c) % PACK
                if c == 0 and t < 2:
                    nc.vector.tensor_copy(h2[t, 0][:], h[t][:, halfc(0)])
                nc.vector.tensor_tensor(dif[:, tv, halfc(c)], h[tv][:].indirect(lists["n3"][:, lc]), h2[tv, c][:], SUB)
            for t in range(PACK):
                nc.vector.scalar_tensor_tensor(o[:, t, halfc(c)], dif[:, t, halfc(c)], -1.0, sig[:, t, halfc(c)], MULT, MULT)
                nc.sync.dma_start(out_rows[:, t, halfc(c)], o[:, t, halfc(c)])
        ob = [sbt("ob0", [P, HALF, PACK], BF16, tag="h3"), sbt("ob1", [P, HALF, PACK], BF16)]

        def interleave(copy, c, lo, hi):
            copy(ob[c][:, lo:hi, :].rearrange("p (c i) t -> p c t i", i=4), o[:, :, c * HALF + lo : c * HALF + hi].rearrange("p t (c i) -> p c t i", i=4))

        ow = sbt("ow", [P, S], I32)

        def planes(c):
            nc.vector.quantize_mx(out=ow[:, halfc(c)].bitcast(FP8X4), scales=osc[:, halfc(c)], in_=ob[c][:].rearrange("p n t -> p (n t)"))
            nc.sync.dma_start(words(out_1)[:, halfc(c)], ow[:, halfc(c)])

        interleave(nc.scalar.copy, 0, 0, HALF)
        interleave(nc.scalar.copy, 1, 0, 64)
        interleave(nc.vector.tensor_copy, 1, 64, HALF)
        planes(0)
        planes(1)
        for r in range(4):
            eng = nc.sync if r == 3 else nc.scalar
            eng.dma_start(out_2[0, r:16:4, :].bitcast(I32), osc[r:P:32, :].bitcast(I32))
